import numpy as np
import ml_dtypes


def mxq(x, axis, fmt="e4m3"):
    dtype, down = {"e4m3": (ml_dtypes.float8_e4m3fn, 7), "e5m2": (ml_dtypes.float8_e5m2, 14)}[fmt]
    v = np.moveaxis(np.asarray(x, np.float32).astype(ml_dtypes.bfloat16).astype(np.float64), axis, -1)
    blocks = v.reshape(v.shape[:-1] + (-1, 32))
    amax = np.abs(blocks).max(-1, keepdims=True)
    byte = np.maximum(np.where(amax > 0, np.frexp(amax)[1] - 1 + 127, 0) - down, 1)
    scale = np.exp2(byte - 127.0)
    codes = (blocks / scale).astype(np.float32).astype(dtype).astype(np.float64)
    return np.moveaxis((codes * scale).reshape(v.shape), -1, axis)


WIDE = False


def mx_kscale(k):
    if not WIDE:
        return np.ones(k)
    levels = np.array([10, -10, 5, -5, 0])
    if k % 512:
        return np.exp2(np.random.permutation(np.resize(levels, k // 32))).repeat(32)
    a = np.empty((k // 512, 16))
    for p in range(k // 512):
        a[p, :8] = np.random.permutation(np.resize(levels, 8))
        for g in range(8):
            far = levels[np.abs(levels - a[p, g]) >= 10]
            a[p, g + 8] = far[np.random.randint(len(far))]
    return np.exp2(a.ravel()).repeat(32)


def f64(x):
    return np.asarray(x).astype(np.float64)


def striped(idx):
    return np.tile(idx.reshape(-1, 16).T, (8, 1)).astype(np.uint16)


def unstriped(offs):
    return offs[:16].T.reshape(-1).astype(np.int64)


def pack_weight(w):
    k, n = w.shape
    w = f64(np.asarray(w, np.float32).astype(ml_dtypes.bfloat16)).reshape(k // 32, 32, n)
    amax = np.abs(w).max(1)
    byte = np.clip(np.where(amax > 0, np.frexp(amax)[1] - 1 + 127 - 7, 1), 1, 254)
    scaled = (w * np.exp2(127.0 - byte)[:, None, :]).reshape(k, n).astype(np.float32)
    words = np.ascontiguousarray(scaled.reshape(k // 512, 128, 4, n).transpose(0, 1, 3, 2)).astype(ml_dtypes.float8_e4m3fn).view(np.uint8)
    return words, np.ascontiguousarray(byte.astype(np.uint8).reshape(k // 512, 16, n))


def unpack_weight(words, scales):
    g, p, n, _ = words.shape
    vals = np.ascontiguousarray(words).view(ml_dtypes.float8_e4m3fn).astype(np.float64) * np.repeat(np.exp2(scales.astype(np.float64) - 127.0), 8, axis=1)[..., None]
    return vals.transpose(0, 1, 3, 2).reshape(g * 512, n)


def planes(y):
    n, m = y.shape
    v = y.astype(np.float32).astype(ml_dtypes.bfloat16).astype(np.float64).reshape(n // 32, 32, m)
    top = np.abs(v).max(1)
    byte = np.clip(np.where(top > 0, np.frexp(top)[1] - 1 + 127 - 7, 1), 1, 254)
    codes = (v * np.exp2(127.0 - byte)[:, None, :]).reshape(n, m).astype(np.float32).astype(ml_dtypes.float8_e4m3fn).view(np.uint8)
    words = codes.reshape(n // 512, 128, 4, m).transpose(0, 1, 3, 2)
    return np.ascontiguousarray(words), np.ascontiguousarray(byte.astype(np.uint8).reshape(n // 512, 16, m))


K, T, S, N, H, W, G, U = 512, 2048, 512, 512, 512, 1024, 1024, 1024


def setup_inputs():
    n = np.random.standard_normal
    s = mx_kscale(K)[:, None]
    u = mx_kscale(H)
    packed_xT = pack_weight(n((K, T)) * s)
    packed_eT = pack_weight(n((K, W)) * s)
    packed_dT = pack_weight(n((K, G)) * s)
    return {
        "x_words": packed_xT[0],
        "x_scales": packed_xT[1],
        "w1": (n((K, N)) / np.sqrt(K) / s).astype(np.float32),
        "e_words": packed_eT[0],
        "e_scales": packed_eT[1],
        "w2": (n((K, N)) / np.sqrt(K) / s).astype(np.float32),
        "d_words": packed_dT[0],
        "d_scales": packed_dT[1],
        "w3": (n((K, N)) / np.sqrt(K) / s).astype(np.float32),
        "unit": (np.random.uniform(0.6, 1.4, (H, 1)) * u[:, None]).astype(np.float32),
        "w4": (n((H, N)) / np.sqrt(H) / u[:, None]).astype(np.float32),
        "offs": striped(np.random.permutation(T)[:S]),
        "prd": striped(np.random.permutation(W)[:S]),
        "shp": striped(np.random.permutation(G)[:S]),
        "fk": striped(np.random.permutation(np.concatenate([np.arange(S), np.random.randint(0, S, U - S)]))),
        "dk1": striped(np.random.permutation(np.concatenate([np.arange(S), np.random.randint(0, S, U - S)]))),
        "dk2": striped(np.random.permutation(np.concatenate([np.arange(S), np.random.randint(0, S, U - S)]))),
    }


def reference(x_words, x_scales, w1, e_words, e_scales, w2, d_words, d_scales, w3, unit, w4, offs, prd, shp, fk, dk1, dk2):
    xq = unpack_weight(x_words, x_scales)[:, unstriped(offs)]
    y = mxq(f64(w1), 0, "e4m3").T @ xq
    ff = y[:, unstriped(fk)]
    e_prd = unpack_weight(e_words, e_scales)[:, unstriped(prd)]
    ye = mxq(f64(w2), 0, "e4m3").T @ e_prd
    pp1 = ye[:, unstriped(dk1)]
    d_shp = unpack_weight(d_words, d_scales)[:, unstriped(shp)]
    yd = mxq(f64(w3), 0, "e4m3").T @ d_shp
    ss1 = yd[:, unstriped(dk2)]
    join = ff * pp1 + 0.7 * ss1
    hid = f64(unit) * np.maximum(join, ff - ss1)
    out_0 = mxq(f64(w4), 0, "e4m3").T @ mxq(hid, 0, "e4m3")
    return (out_0,) + planes(out_0)

@@ -1,0 +1,268 @@
+from contextlib import ExitStack
+
+import concourse.mybir as mybir
+from concourse.masks import make_identity
+
+K, T, S, N, H, W, G, U = 512, 2048, 512, 512, 512, 1024, 1024, 1024
+FLOPS = 2 * (3 * K * H * S + H * N * U)
+
+F32 = mybir.dt.float32
+BF16 = mybir.dt.bfloat16
+I32 = mybir.dt.int32
+U32 = mybir.dt.uint32
+U16 = mybir.dt.uint16
+U8 = mybir.dt.uint8
+FP8X4 = mybir.dt.float8_e4m3fn_x4
+ALU = mybir.AluOpType
+COPY = mybir.ActivationFunctionType.Copy
+
+P = 128
+PACK = 4
+HALF = 256
+SHOP = 0.7
+CHUNKS = (256, 256, 256, 128, 128)
+TAIL = 2
+
+
+def tile_picked_ystarjn_max_po_kernel(
+    tc, x_words, x_scales, w1, e_words, e_scales, w2, d_words, d_scales, w3, unit, w4,
+    offs, prd, shp, fk, dk1, dk2, out_0, out_1, out_2,
+):
+    nc = tc.nc
+    with ExitStack() as ctx:
+        keep = ctx.enter_context(tc.tile_pool(name="keep", bufs=1))
+        ring = ctx.enter_context(tc.tile_pool(name="ring", bufs=2))
+        psum = ctx.enter_context(tc.psum_pool(name="psum", bufs=2))
+
+        def load_list(name, src):
+            tile = keep.tile(list(src.shape), U16, name=name)
+            nc.sync.dma_start(tile[:], src)
+            return tile
+
+        def load_words(name, src):
+            tile = keep.tile([P, src.shape[2]], U32, name=name)
+            nc.sync.dma_start(tile[:].bitcast(I32), src[0].rearrange("p c t -> p (c t)").bitcast(I32))
+            return tile
+
+        def clear_scales(name, src, engine):
+            tile = keep.tile([P, src.shape[2]], U8, name=name)
+            engine.memset(tile[:].bitcast(I32), 0)
+            return tile
+
+        def load_scales(tile, src, queue):
+            for q in range(4):
+                queue.dma_start(tile[32 * q : 32 * q + 4, :].bitcast(I32), src[0, 4 * q : 4 * q + 4, :].bitcast(I32))
+
+        def load_weight(name, src, cols):
+            tile = keep.tile([P, PACK, cols.stop - cols.start], F32, name=name)
+            nc.sync.dma_start(tile[:], src.rearrange("(p j) c -> p j c", j=PACK)[:, :, cols])
+            return tile
+
+        e_table = clear_scales("e_table", e_scales, nc.vector)
+        d_table = clear_scales("d_table", d_scales, nc.gpsimd)
+        load_scales(d_table, d_scales, nc.gpsimd)
+        x_table = clear_scales("x_table", x_scales, nc.vector)
+        load_scales(x_table, x_scales, nc.gpsimd)
+
+        lo, hi = slice(0, HALF), slice(HALF, 2 * HALF)
+        prd_sb = load_list("prd_sb", prd)
+        e_sb = load_words("e_sb", e_words)
+        w2_raw = [load_weight("w2_lo", w2, lo)]
+        load_scales(e_table, e_scales, nc.sync)
+        unit_rows = keep.tile([P, PACK], F32)
+        with nc.allow_non_contiguous_dma(reason="one value a partition and tile"):
+            nc.sync.dma_start(unit_rows[:], unit.rearrange("(t p) o -> p (t o)", p=P))
+        d_sb = load_words("d_sb", d_words)
+        shp_sb = load_list("shp_sb", shp)
+        w3_raw = [load_weight("w3_lo", w3, lo)]
+        dk1_sb = load_list("dk1_sb", dk1)
+        x_sb = load_words("x_sb", x_words)
+        offs_sb = load_list("offs_sb", offs)
+        w1_raw = [load_weight("w1_lo", w1, lo)]
+        dk2_sb = load_list("dk2_sb", dk2)
+        w2_raw.append(load_weight("w2_hi", w2, hi))
+        fk_sb = load_list("fk_sb", fk)
+        w3_raw.append(load_weight("w3_hi", w3, hi))
+        w1_raw.append(load_weight("w1_hi", w1, hi))
+        w4_raw = load_weight("w4_raw", w4, slice(0, N))
+        unit_words = keep.tile([P, PACK], F32)
+        nc.sync.dma_start(unit_words[:], unit.rearrange("(p j) o -> p (j o)", j=PACK))
+
+        negated = keep.tile([P, PACK], F32)
+        nc.vector.tensor_scalar(negated[:], unit_rows[:], -SHOP, None, ALU.mult)
+        shop_gain = keep.tile([P, PACK], F32)
+        nc.vector.scalar_tensor_tensor(shop_gain[:], unit_rows[:], SHOP, negated[:], ALU.mult, ALU.max)
+        fact_gain = keep.tile([P, PACK], F32)
+        nc.vector.scalar_tensor_tensor(fact_gain[:], unit_rows[:], SHOP, negated[:], ALU.mult, ALU.min)
+
+        def pick(name, words, scales, offsets):
+            codes = keep.tile([P, S], U32, name=name + "_codes", align_bytes=64)
+            plane = keep.tile([P, S], U8, name=name + "_plane", align_bytes=64)
+            nc.vector.tensor_copy(codes[:], words[:].indirect(offsets[:]))
+            nc.vector.tensor_copy(plane[:], scales[:].indirect(offsets[:]))
+            return codes, plane
+
+        def round_on(engine, out, in_):
+            if engine == "gpsimd":
+                nc.gpsimd.tensor_scalar(out, in_, 1.0, 0.0, ALU.mult, ALU.add)
+            elif engine == "scalar":
+                nc.scalar.copy(out, in_)
+            else:
+                nc.vector.tensor_copy(out, in_)
+
+        def windows(name, raw, picked, gain, half, cast_engine, out_engine):
+            grouped = ring.tile([P, HALF * PACK], BF16, name="w_grouped", align_bytes=64, bufs=3)
+            round_on(
+                cast_engine,
+                grouped[:].rearrange("p (c i j) -> p c j i", i=4, j=PACK),
+                raw[:].rearrange("p j (c i) -> p c j i", i=4),
+            )
+            codes = keep.tile([P, HALF], U32, name=name + "_wc", align_bytes=64)
+            plane = keep.tile([P, HALF], U8, name=name + "_wp", align_bytes=64)
+            nc.vector.quantize_mx(out=codes[:].bitcast(FP8X4), scales=plane[:], in_=grouped[:])
+            tiles = []
+            for s in range(2):
+                t = 2 * half + s
+                cols = slice(s * P, (s + 1) * P)
+                bank = psum.tile([P, S], F32, name="product", bufs=3)
+                nc.tensor.matmul_mx(
+                    out=bank[:], lhsT=codes[:, cols].bitcast(FP8X4), lhsT_scale=plane[:, cols],
+                    rhs=picked[0][:].bitcast(FP8X4), rhs_scale=picked[1][:], start=True, stop=True,
+                )
+                window = keep.tile([P, S], F32, name="%s_window%d" % (name, t))
+                factor = gain if isinstance(gain, float) else gain[:, t : t + 1]
+                if out_engine == "scalar":
+                    nc.scalar.activation(window[:], bank[:], COPY, scale=factor)
+                else:
+                    nc.vector.tensor_scalar(window[:], bank[:], factor, None, ALU.mult)
+                tiles.append(window)
+            return tiles
+
+        e_pick = pick("e", e_sb, e_table, prd_sb)
+        goods = windows("w2a", w2_raw[0], e_pick, -1.0 / SHOP, 0, "scalar", "scalar")
+        d_pick = pick("d", d_sb, d_table, shp_sb)
+        shops = windows("w3a", w3_raw[0], d_pick, shop_gain, 0, "scalar", "scalar")
+        x_pick = pick("x", x_sb, x_table, offs_sb)
+        facts = windows("w1a", w1_raw[0], x_pick, fact_gain, 0, "vector", "vector")
+        goods = goods + windows("w2b", w2_raw[1], e_pick, -1.0 / SHOP, 1, "vector", "vector")
+        shops = shops + windows("w3b", w3_raw[1], d_pick, shop_gain, 1, "vector", "vector")
+        facts = facts + windows("w1b", w1_raw[1], x_pick, fact_gain, 1, "vector", "vector")
+
+        identity = keep.tile([P, P], F32)
+        make_identity(nc, identity[:])
+        twice = keep.tile([P, PACK], F32)
+        nc.gpsimd.tensor_scalar(twice[:], unit_words[:], 0.0, 2.0, ALU.is_ge, ALU.mult)
+        signs = keep.tile([P, 2, 2], BF16)
+        nc.gpsimd.tensor_scalar(signs[:].rearrange("p u e -> p (u e)"), twice[:], 1.0, -1.0, ALU.mult, ALU.add)
+
+        out_codes = keep.tile([P, U], U32, align_bytes=64)
+        out_plane = keep.tile([P, U], U8, align_bytes=64)
+        w4_codes = keep.tile([P, N], U32, align_bytes=64)
+        w4_plane = keep.tile([P, N], U8, align_bytes=64)
+
+        def quantise_w4():
+            grouped = keep.tile([P, N * PACK], BF16, name="w4_grouped", align_bytes=64)
+            round_on(
+                "vector",
+                grouped[:].rearrange("p (t m j) -> p m j t", t=4, j=PACK),
+                w4_raw[:].rearrange("p j (m t) -> p m j t", t=4),
+            )
+            nc.vector.quantize_mx(out=w4_codes[:].bitcast(FP8X4), scales=w4_plane[:], in_=grouped[:])
+
+        def add_turned(bank_cols, first, second):
+            nc.tensor.matmul(bank_cols, first, identity[:], start=True, stop=False, is_transpose=True)
+            nc.tensor.matmul(bank_cols, second, identity[:], start=False, stop=True, is_transpose=True)
+
+        def join_half(start, width, half, larger, tail):
+            entries = slice(start // 16, (start + width) // 16)
+            name = "_%d_%d" % (start, half)
+            fact = keep.tile([P, 2, width], F32, name="fact" + name)
+            shop = keep.tile([P, 2, width], F32, name="shop" + name)
+            good = keep.tile([P, 2, width], F32, name="good" + name)
+            for s in range(2):
+                nc.scalar.activation(good[:, s, :], goods[2 * half + s][:].indirect(dk1_sb[:, entries]), COPY)
+            for s in range(2):
+                nc.scalar.activation(fact[:, s, :], facts[2 * half + s][:].indirect(fk_sb[:, entries]), COPY)
+            for s in range(2):
+                nc.scalar.activation(shop[:, s, :], shops[2 * half + s][:].indirect(dk2_sb[:, entries]), COPY)
+            nc.gpsimd.tensor_tensor(good[:], good[:], fact[:], ALU.mult)
+            blocks = width // P
+            joined = psum.tile([P, blocks, 2, P], F32, name="joined")
+            differ = psum.tile([P, blocks, 2, P], F32, name="differ")
+            for b in range(blocks):
+                for s in range(2):
+                    add_turned(differ[:, b, s, :], fact[:, s, b * P : (b + 1) * P], shop[:, s, b * P : (b + 1) * P])
+            for b in range(blocks):
+                for s in range(2):
+                    add_turned(joined[:, b, s, :], good[:, s, b * P : (b + 1) * P], shop[:, s, b * P : (b + 1) * P])
+            order = "p b s (q u e) -> p u b (s q) e"
+            less = ring.tile([P, 2, blocks, 64, 2], F32, name="less")
+            if tail:
+                nc.scalar.activation(less[:], differ[:].rearrange(order, u=2, e=2), COPY, scale=-1.0 / SHOP)
+            else:
+                nc.vector.tensor_scalar(less[:], differ[:].rearrange(order, u=2, e=2), -1.0 / SHOP, None, ALU.mult)
+            nc.vector.tensor_tensor(
+                larger[:, :, :, half * P : (half + 1) * P].rearrange("p u b (q e) -> p u b q e", e=2),
+                joined[:].rearrange(order, u=2, e=2),
+                less[:],
+                ALU.max,
+            )
+
+        def finish(start, width, larger, tail):
+            blocks = width // P
+            back = psum.tile([P, 2, width], F32, name="back", bufs=1)
+            for b in range(blocks):
+                for u in range(2):
+                    nc.tensor.transpose(back[:, u, b * P : (b + 1) * P], larger[:, u, b, :].bitcast(F32), identity[:])
+            hid = ring.tile([P, width * PACK], BF16, name="hid", align_bytes=64)
+            nc.vector.tensor_tensor(
+                hid[:].rearrange("p (r u e) -> p r u e", u=2, e=2),
+                back[:].bitcast(BF16).rearrange("p u (r e) -> p r u e", e=2),
+                signs[:].unsqueeze(1).to_broadcast([P, width, 2, 2]),
+                ALU.mult,
+            )
+            codes = ring.tile([P, width], U32, name="hid_codes", align_bytes=64)
+            plane = ring.tile([P, width], U8, name="hid_plane", align_bytes=64)
+            nc.vector.quantize_mx(out=codes[:].bitcast(FP8X4), scales=plane[:], in_=hid[:])
+            result = ring.tile([P, PACK, width], F32, name="result", bufs=3)
+            per_bank = S // width
+            for g in range(PACK // per_bank):
+                bank = psum.tile([P, per_bank, width], F32, name="product", bufs=3)
+                for s in range(per_bank):
+                    cols = slice((g * per_bank + s) * P, (g * per_bank + s + 1) * P)
+                    nc.tensor.matmul_mx(
+                        out=bank[:, s, :], lhsT=w4_codes[:, cols].bitcast(FP8X4), lhsT_scale=w4_plane[:, cols],
+                        rhs=codes[:].bitcast(FP8X4), rhs_scale=plane[:], start=True, stop=True,
+                    )
+                part = result[:, g * per_bank : (g + 1) * per_bank, :]
+                if tail:
+                    nc.scalar.copy(part, bank[:])
+                else:
+                    nc.vector.tensor_copy(part, bank[:])
+            cols = slice(start, start + width)
+            nc.sync.dma_start(out_0.rearrange("(p t) r -> p t r", t=PACK)[:, :, cols], result[:])
+            rounded = ring.tile([P, width * PACK], BF16, name="rounded", align_bytes=64)
+            round_on(
+                "vector",
+                rounded[:].rearrange("p (c i t) -> p c t i", i=4, t=PACK),
+                result[:].rearrange("p t (c i) -> p c t i", i=4),
+            )
+            nc.vector.quantize_mx(out=out_codes[:, cols].bitcast(FP8X4), scales=out_plane[:, cols], in_=rounded[:])
+            nc.sync.dma_start(
+                out_1[0].rearrange("p c t -> p (c t)")[:, PACK * start : PACK * (start + width)].bitcast(I32),
+                out_codes[:, cols].bitcast(I32),
+            )
+
+        start = 0
+        for c, width in enumerate(CHUNKS):
+            tail = c >= len(CHUNKS) - TAIL
+            larger = ring.tile([P, 2, width // P, 2 * P], BF16, name="larger")
+            for half in range(2):
+                join_half(start, width, half, larger, tail)
+            if c == 0:
+                quantise_w4()
+            finish(start, width, larger, tail)
+            start = start + width
+        for q in range(4):
+            queue = nc.sync if q % 2 == 0 else nc.scalar
+            queue.dma_start(out_2[0, 4 * q : 4 * q + 4, :].bitcast(I32), out_plane[32 * q : 32 * q + 4, :].bitcast(I32))

@@ -1,7 +1,6 @@
 from contextlib import ExitStack
 
 import concourse.mybir as mybir
-from concourse.masks import make_identity
 
 K, T, S, N, H, W, G, U = 512, 2048, 512, 512, 512, 1024, 1024, 1024
 FLOPS = 2 * (3 * K * H * S + H * N * U)
@@ -18,10 +17,12 @@ COPY = mybir.ActivationFunctionType.Copy
 
 P = 128
 PACK = 4
-HALF = 256
 SHOP = 0.7
-CHUNKS = (256, 256, 256, 128, 128)
-TAIL = 2
+SPARE = 16
+CHUNKS = (512, 256, 128, 128)
+FUSED = ()
+VCAST = ()
+VEVAC = ()
 
 
 def tile_picked_ystarjn_max_po_kernel(
@@ -53,47 +54,47 @@ def tile_picked_ystarjn_max_po_kernel(
             for q in range(4):
                 queue.dma_start(tile[32 * q : 32 * q + 4, :].bitcast(I32), src[0, 4 * q : 4 * q + 4, :].bitcast(I32))
 
-        def load_weight(name, src, cols):
-            tile = keep.tile([P, PACK, cols.stop - cols.start], F32, name=name)
-            nc.sync.dma_start(tile[:], src.rearrange("(p j) c -> p j c", j=PACK)[:, :, cols])
-            return tile
+        def load_weight(name, src, parts):
+            tiles = []
+            width = N // parts
+            for n in range(parts):
+                tile = keep.tile([P, PACK, width], F32, name="%s%d" % (name, n))
+                nc.sync.dma_start(tile[:], src.rearrange("(p j) c -> p j c", j=PACK)[:, :, n * width : (n + 1) * width])
+                tiles.append(tile)
+            return tiles
 
-        e_table = clear_scales("e_table", e_scales, nc.vector)
-        d_table = clear_scales("d_table", d_scales, nc.gpsimd)
-        load_scales(d_table, d_scales, nc.gpsimd)
+        d_table = clear_scales("d_table", d_scales, nc.vector)
         x_table = clear_scales("x_table", x_scales, nc.vector)
-        load_scales(x_table, x_scales, nc.gpsimd)
-
-        lo, hi = slice(0, HALF), slice(HALF, 2 * HALF)
-        prd_sb = load_list("prd_sb", prd)
-        e_sb = load_words("e_sb", e_words)
-        w2_raw = [load_weight("w2_lo", w2, lo)]
-        load_scales(e_table, e_scales, nc.sync)
-        unit_rows = keep.tile([P, PACK], F32)
-        with nc.allow_non_contiguous_dma(reason="one value a partition and tile"):
-            nc.sync.dma_start(unit_rows[:], unit.rearrange("(t p) o -> p (t o)", p=P))
+        e_table = clear_scales("e_table", e_scales, nc.gpsimd)
+        load_scales(e_table, e_scales, nc.gpsimd)
+        unit_sb = keep.tile([P, PACK], F32)
+        nc.scalar.dma_start(unit_sb[:], unit.rearrange("(p t) o -> p (t o)", t=PACK))
         d_sb = load_words("d_sb", d_words)
         shp_sb = load_list("shp_sb", shp)
-        w3_raw = [load_weight("w3_lo", w3, lo)]
-        dk1_sb = load_list("dk1_sb", dk1)
+        load_scales(d_table, d_scales, nc.sync)
+        w3_raw = load_weight("w3_raw", w3, 2)
+        dk2_sb = load_list("dk2_sb", dk2)
         x_sb = load_words("x_sb", x_words)
         offs_sb = load_list("offs_sb", offs)
-        w1_raw = [load_weight("w1_lo", w1, lo)]
-        dk2_sb = load_list("dk2_sb", dk2)
-        w2_raw.append(load_weight("w2_hi", w2, hi))
+        load_scales(x_table, x_scales, nc.sync)
+        w1_raw = load_weight("w1_raw", w1, 2)
         fk_sb = load_list("fk_sb", fk)
-        w3_raw.append(load_weight("w3_hi", w3, hi))
-        w1_raw.append(load_weight("w1_hi", w1, hi))
-        w4_raw = load_weight("w4_raw", w4, slice(0, N))
-        unit_words = keep.tile([P, PACK], F32)
-        nc.sync.dma_start(unit_words[:], unit.rearrange("(p j) o -> p (j o)", j=PACK))
+        e_sb = load_words("e_sb", e_words)
+        prd_sb = load_list("prd_sb", prd)
+        w2_raw = load_weight("w2_raw", w2, 2)
+        dk1_sb = load_list("dk1_sb", dk1)
+        w4_raw = load_weight("w4_raw", w4, 1)
 
         negated = keep.tile([P, PACK], F32)
-        nc.vector.tensor_scalar(negated[:], unit_rows[:], -SHOP, None, ALU.mult)
-        shop_gain = keep.tile([P, PACK], F32)
-        nc.vector.scalar_tensor_tensor(shop_gain[:], unit_rows[:], SHOP, negated[:], ALU.mult, ALU.max)
+        nc.scalar.activation(negated[:], unit_sb[:], COPY, scale=-1.0)
         fact_gain = keep.tile([P, PACK], F32)
-        nc.vector.scalar_tensor_tensor(fact_gain[:], unit_rows[:], SHOP, negated[:], ALU.mult, ALU.min)
+        nc.vector.tensor_tensor(fact_gain[:], unit_sb[:], negated[:], ALU.max)
+        shop_gain = keep.tile([P, PACK], F32)
+        nc.vector.tensor_tensor(shop_gain[:], unit_sb[:], negated[:], ALU.min)
+        twice = keep.tile([P, PACK], F32)
+        nc.gpsimd.tensor_scalar(twice[:], unit_sb[:], 0.0, 2.0, ALU.is_ge, ALU.mult)
+        signs = keep.tile([P, PACK], F32)
+        nc.gpsimd.tensor_scalar(signs[:], twice[:], 1.0, -1.0, ALU.mult, ALU.add)
 
         def pick(name, words, scales, offsets):
             codes = keep.tile([P, S], U32, name=name + "_codes", align_bytes=64)
@@ -102,151 +103,108 @@ def tile_picked_ystarjn_max_po_kernel(
             nc.vector.tensor_copy(plane[:], scales[:].indirect(offsets[:]))
             return codes, plane
 
-        def round_on(engine, out, in_):
-            if engine == "gpsimd":
-                nc.gpsimd.tensor_scalar(out, in_, 1.0, 0.0, ALU.mult, ALU.add)
-            elif engine == "scalar":
-                nc.scalar.copy(out, in_)
-            else:
-                nc.vector.tensor_copy(out, in_)
-
-        def windows(name, raw, picked, gain, half, cast_engine, out_engine):
-            grouped = ring.tile([P, HALF * PACK], BF16, name="w_grouped", align_bytes=64, bufs=3)
-            round_on(
-                cast_engine,
-                grouped[:].rearrange("p (c i j) -> p c j i", i=4, j=PACK),
-                raw[:].rearrange("p j (c i) -> p c j i", i=4),
-            )
-            codes = keep.tile([P, HALF], U32, name=name + "_wc", align_bytes=64)
-            plane = keep.tile([P, HALF], U8, name=name + "_wp", align_bytes=64)
+        def quantise(name, raws, engines):
+            grouped = ring.tile([P, N * PACK], BF16, name="w_grouped", align_bytes=64)
+            share = P // len(raws)
+            for n, raw in enumerate(raws):
+                dealt = grouped[:].rearrange("p (t m j) -> p m j t", t=PACK, j=PACK)[:, n * share : (n + 1) * share, :, :]
+                source = raw[:].rearrange("p j (m t) -> p m j t", t=PACK)
+                if engines[n] == "x":
+                    nc.vector.tensor_tensor(dealt, source, signs[:].unsqueeze(1).unsqueeze(3).to_broadcast([P, share, PACK, PACK]), ALU.mult)
+                elif engines[n] == "s":
+                    nc.scalar.copy(dealt, source)
+                elif engines[n] == "g":
+                    nc.gpsimd.tensor_copy(dealt, source)
+                else:
+                    nc.vector.tensor_copy(dealt, source)
+            codes = keep.tile([P, N], U32, name=name + "_wc", align_bytes=64)
+            plane = keep.tile([P, N], U8, name=name + "_wp", align_bytes=64)
             nc.vector.quantize_mx(out=codes[:].bitcast(FP8X4), scales=plane[:], in_=grouped[:])
+            return codes, plane
+
+        def windows(name, weight, picked, gain, engines):
             tiles = []
-            for s in range(2):
-                t = 2 * half + s
-                cols = slice(s * P, (s + 1) * P)
-                bank = psum.tile([P, S], F32, name="product", bufs=3)
+            for t in range(PACK):
+                cols = slice(t * P, (t + 1) * P)
+                bank = psum.tile([P, S], F32, name="product", bufs=4)
                 nc.tensor.matmul_mx(
-                    out=bank[:], lhsT=codes[:, cols].bitcast(FP8X4), lhsT_scale=plane[:, cols],
+                    out=bank[:], lhsT=weight[0][:, cols].bitcast(FP8X4), lhsT_scale=weight[1][:, cols],
                     rhs=picked[0][:].bitcast(FP8X4), rhs_scale=picked[1][:], start=True, stop=True,
                 )
-                window = keep.tile([P, S], F32, name="%s_window%d" % (name, t))
-                factor = gain if isinstance(gain, float) else gain[:, t : t + 1]
-                if out_engine == "scalar":
-                    nc.scalar.activation(window[:], bank[:], COPY, scale=factor)
+                window = keep.tile([P, S + SPARE], F32, name="%s_window%d" % (name, t))
+                if SPARE:
+                    nc.gpsimd.memset(window[:, S:], 0.0)
+                if gain is None:
+                    if engines[t] == "s":
+                        nc.scalar.activation(window[:, :S], bank[:], COPY)
+                    else:
+                        nc.vector.tensor_copy(window[:, :S], bank[:])
+                elif engines[t] == "s":
+                    nc.scalar.activation(window[:, :S], bank[:], COPY, scale=gain[:, t : t + 1])
                 else:
-                    nc.vector.tensor_scalar(window[:], bank[:], factor, None, ALU.mult)
+                    nc.vector.tensor_scalar(window[:, :S], bank[:], gain[:, t : t + 1], None, ALU.mult)
                 tiles.append(window)
             return tiles
 
-        e_pick = pick("e", e_sb, e_table, prd_sb)
-        goods = windows("w2a", w2_raw[0], e_pick, -1.0 / SHOP, 0, "scalar", "scalar")
         d_pick = pick("d", d_sb, d_table, shp_sb)
-        shops = windows("w3a", w3_raw[0], d_pick, shop_gain, 0, "scalar", "scalar")
+        shops = windows("shop", quantise("w3", w3_raw, "sv"), d_pick, shop_gain, "ssss")
         x_pick = pick("x", x_sb, x_table, offs_sb)
-        facts = windows("w1a", w1_raw[0], x_pick, fact_gain, 0, "vector", "vector")
-        goods = goods + windows("w2b", w2_raw[1], e_pick, -1.0 / SHOP, 1, "vector", "vector")
-        shops = shops + windows("w3b", w3_raw[1], d_pick, shop_gain, 1, "vector", "vector")
-        facts = facts + windows("w1b", w1_raw[1], x_pick, fact_gain, 1, "vector", "vector")
-
-        identity = keep.tile([P, P], F32)
-        make_identity(nc, identity[:])
-        twice = keep.tile([P, PACK], F32)
-        nc.gpsimd.tensor_scalar(twice[:], unit_words[:], 0.0, 2.0, ALU.is_ge, ALU.mult)
-        signs = keep.tile([P, 2, 2], BF16)
-        nc.gpsimd.tensor_scalar(signs[:].rearrange("p u e -> p (u e)"), twice[:], 1.0, -1.0, ALU.mult, ALU.add)
+        facts = windows("fact", quantise("w1", w1_raw, "vv"), x_pick, fact_gain, "ssss")
+        e_pick = pick("e", e_sb, e_table, prd_sb)
+        goods = windows("good", quantise("w2", w2_raw, "vv"), e_pick, None, "ssss")
 
         out_codes = keep.tile([P, U], U32, align_bytes=64)
         out_plane = keep.tile([P, U], U8, align_bytes=64)
-        w4_codes = keep.tile([P, N], U32, align_bytes=64)
-        w4_plane = keep.tile([P, N], U8, align_bytes=64)
 
-        def quantise_w4():
-            grouped = keep.tile([P, N * PACK], BF16, name="w4_grouped", align_bytes=64)
-            round_on(
-                "vector",
-                grouped[:].rearrange("p (t m j) -> p m j t", t=4, j=PACK),
-                w4_raw[:].rearrange("p j (m t) -> p m j t", t=4),
-            )
-            nc.vector.quantize_mx(out=w4_codes[:].bitcast(FP8X4), scales=w4_plane[:], in_=grouped[:])
-
-        def add_turned(bank_cols, first, second):
-            nc.tensor.matmul(bank_cols, first, identity[:], start=True, stop=False, is_transpose=True)
-            nc.tensor.matmul(bank_cols, second, identity[:], start=False, stop=True, is_transpose=True)
-
-        def join_half(start, width, half, larger, tail):
+        def join(c, start, width):
             entries = slice(start // 16, (start + width) // 16)
-            name = "_%d_%d" % (start, half)
-            fact = keep.tile([P, 2, width], F32, name="fact" + name)
-            shop = keep.tile([P, 2, width], F32, name="shop" + name)
-            good = keep.tile([P, 2, width], F32, name="good" + name)
-            for s in range(2):
-                nc.scalar.activation(good[:, s, :], goods[2 * half + s][:].indirect(dk1_sb[:, entries]), COPY)
-            for s in range(2):
-                nc.scalar.activation(fact[:, s, :], facts[2 * half + s][:].indirect(fk_sb[:, entries]), COPY)
-            for s in range(2):
-                nc.scalar.activation(shop[:, s, :], shops[2 * half + s][:].indirect(dk2_sb[:, entries]), COPY)
-            nc.gpsimd.tensor_tensor(good[:], good[:], fact[:], ALU.mult)
-            blocks = width // P
-            joined = psum.tile([P, blocks, 2, P], F32, name="joined")
-            differ = psum.tile([P, blocks, 2, P], F32, name="differ")
-            for b in range(blocks):
-                for s in range(2):
-                    add_turned(differ[:, b, s, :], fact[:, s, b * P : (b + 1) * P], shop[:, s, b * P : (b + 1) * P])
-            for b in range(blocks):
-                for s in range(2):
-                    add_turned(joined[:, b, s, :], good[:, s, b * P : (b + 1) * P], shop[:, s, b * P : (b + 1) * P])
-            order = "p b s (q u e) -> p u b (s q) e"
-            less = ring.tile([P, 2, blocks, 64, 2], F32, name="less")
-            if tail:
-                nc.scalar.activation(less[:], differ[:].rearrange(order, u=2, e=2), COPY, scale=-1.0 / SHOP)
-            else:
-                nc.vector.tensor_scalar(less[:], differ[:].rearrange(order, u=2, e=2), -1.0 / SHOP, None, ALU.mult)
-            nc.vector.tensor_tensor(
-                larger[:, :, :, half * P : (half + 1) * P].rearrange("p u b (q e) -> p u b q e", e=2),
-                joined[:].rearrange(order, u=2, e=2),
-                less[:],
-                ALU.max,
-            )
-
-        def finish(start, width, larger, tail):
-            blocks = width // P
-            back = psum.tile([P, 2, width], F32, name="back", bufs=1)
-            for b in range(blocks):
-                for u in range(2):
-                    nc.tensor.transpose(back[:, u, b * P : (b + 1) * P], larger[:, u, b, :].bitcast(F32), identity[:])
+            fact = ring.tile([P, PACK, width], F32, name="fact", bufs=2)
+            less = ring.tile([P, PACK, width], F32, name="less", bufs=2)
+            more = ring.tile([P, PACK, width], F32, name="more", bufs=2)
+            for t in range(PACK):
+                nc.scalar.activation(fact[:, t, :], facts[t][:].indirect(fk_sb[:, entries]), COPY)
+            for t in range(PACK):
+                nc.scalar.activation(less[:, t, :], shops[t][:].indirect(dk2_sb[:, entries]), COPY)
+            for t in range(PACK):
+                nc.vector.tensor_tensor(more[:, t, :], goods[t][:].indirect(dk1_sb[:, entries]), fact[:, t, :], ALU.mult)
+            nc.vector.scalar_tensor_tensor(more[:], less[:], -SHOP, more[:], ALU.mult, ALU.add)
+            nc.vector.tensor_tensor(less[:], less[:], fact[:], ALU.add)
             hid = ring.tile([P, width * PACK], BF16, name="hid", align_bytes=64)
+            walk = "p t (c i) -> p c t i"
             nc.vector.tensor_tensor(
-                hid[:].rearrange("p (r u e) -> p r u e", u=2, e=2),
-                back[:].bitcast(BF16).rearrange("p u (r e) -> p r u e", e=2),
-                signs[:].unsqueeze(1).to_broadcast([P, width, 2, 2]),
-                ALU.mult,
+                hid[:].rearrange("p (c i t) -> p c t i", i=4, t=PACK), more[:].rearrange(walk, i=4), less[:].rearrange(walk, i=4), ALU.max
             )
             codes = ring.tile([P, width], U32, name="hid_codes", align_bytes=64)
             plane = ring.tile([P, width], U8, name="hid_plane", align_bytes=64)
             nc.vector.quantize_mx(out=codes[:].bitcast(FP8X4), scales=plane[:], in_=hid[:])
-            result = ring.tile([P, PACK, width], F32, name="result", bufs=3)
-            per_bank = S // width
-            for g in range(PACK // per_bank):
-                bank = psum.tile([P, per_bank, width], F32, name="product", bufs=3)
-                for s in range(per_bank):
-                    cols = slice((g * per_bank + s) * P, (g * per_bank + s + 1) * P)
+            return codes, plane
+
+        def finish(c, start, width, codes, plane):
+            result = ring.tile([P, PACK, width], F32, name="result", bufs=2)
+            rounded = ring.tile([P, width * PACK], BF16, name="rounded", align_bytes=64)
+            for b in range(width // P):
+                cols = slice(b * P, (b + 1) * P)
+                bank = psum.tile([P, PACK, P], F32, name="measure", bufs=4)
+                for t in range(PACK):
+                    rows = slice(t * P, (t + 1) * P)
                     nc.tensor.matmul_mx(
-                        out=bank[:, s, :], lhsT=w4_codes[:, cols].bitcast(FP8X4), lhsT_scale=w4_plane[:, cols],
-                        rhs=codes[:].bitcast(FP8X4), rhs_scale=plane[:], start=True, stop=True,
+                        out=bank[:, t, :], lhsT=w4_q[0][:, rows].bitcast(FP8X4), lhsT_scale=w4_q[1][:, rows],
+                        rhs=codes[:, cols].bitcast(FP8X4), rhs_scale=plane[:, cols], start=True, stop=True,
                     )
-                part = result[:, g * per_bank : (g + 1) * per_bank, :]
-                if tail:
-                    nc.scalar.copy(part, bank[:])
+                if c not in VCAST:
+                    nc.scalar.copy(
+                        rounded[:, b * S : (b + 1) * S].rearrange("p (r t) -> p r t", t=PACK), bank[:].rearrange("p t r -> p r t")
+                    )
+                if c in VEVAC:
+                    nc.vector.tensor_copy(result[:, :, cols], bank[:])
                 else:
-                    nc.vector.tensor_copy(part, bank[:])
+                    nc.scalar.copy(result[:, :, cols], bank[:])
             cols = slice(start, start + width)
             nc.sync.dma_start(out_0.rearrange("(p t) r -> p t r", t=PACK)[:, :, cols], result[:])
-            rounded = ring.tile([P, width * PACK], BF16, name="rounded", align_bytes=64)
-            round_on(
-                "vector",
-                rounded[:].rearrange("p (c i t) -> p c t i", i=4, t=PACK),
-                result[:].rearrange("p t (c i) -> p c t i", i=4),
-            )
+            if c in VCAST:
+                nc.vector.tensor_copy(
+                    rounded[:].rearrange("p (c i t) -> p c t i", i=4, t=PACK), result[:].rearrange("p t (c i) -> p c t i", i=4)
+                )
             nc.vector.quantize_mx(out=out_codes[:, cols].bitcast(FP8X4), scales=out_plane[:, cols], in_=rounded[:])
             nc.sync.dma_start(
                 out_1[0].rearrange("p c t -> p (c t)")[:, PACK * start : PACK * (start + width)].bitcast(I32),
@@ -255,13 +213,10 @@ def tile_picked_ystarjn_max_po_kernel(
 
         start = 0
         for c, width in enumerate(CHUNKS):
-            tail = c >= len(CHUNKS) - TAIL
-            larger = ring.tile([P, 2, width // P, 2 * P], BF16, name="larger")
-            for half in range(2):
-                join_half(start, width, half, larger, tail)
+            codes, plane = join(c, start, width)
             if c == 0:
-                quantise_w4()
-            finish(start, width, larger, tail)
+                w4_q = quantise("w4", w4_raw, "x")
+            finish(c, start, width, codes, plane)
             start = start + width
         for q in range(4):
             queue = nc.sync if q % 2 == 0 else nc.scalar

@@ -2,7 +2,7 @@ from contextlib import ExitStack
 
 import concourse.mybir as mybir
 
-K, T, S, N, H, W, G, U = 512, 2048, 512, 512, 512, 1024, 1024, 1024
+K, S, N, H, U = 512, 512, 512, 512, 1024
 FLOPS = 2 * (3 * K * H * S + H * N * U)
 
 F32 = mybir.dt.float32
@@ -17,12 +17,15 @@ COPY = mybir.ActivationFunctionType.Copy
 
 P = 128
 PACK = 4
+LINE = 4
+LIST_ROWS = 16
+QUADRANTS = 4
 SHOP = 0.7
 SPARE = 16
-CHUNKS = (512, 256, 128, 128)
-FUSED = ()
-VCAST = ()
-VEVAC = ()
+HALVES = 2
+CHUNKS = (256, 512, 128, 128)
+STORE_BLOCKS = 2
+GOODS_BANKS_ON_VECTOR = 3
 
 
 def tile_picked_ystarjn_max_po_kernel(
@@ -33,7 +36,7 @@ def tile_picked_ystarjn_max_po_kernel(
     with ExitStack() as ctx:
         keep = ctx.enter_context(tc.tile_pool(name="keep", bufs=1))
         ring = ctx.enter_context(tc.tile_pool(name="ring", bufs=2))
-        psum = ctx.enter_context(tc.psum_pool(name="psum", bufs=2))
+        psum = ctx.enter_context(tc.psum_pool(name="psum", bufs=4))
 
         def load_list(name, src):
             tile = keep.tile(list(src.shape), U16, name=name)
@@ -42,16 +45,16 @@ def tile_picked_ystarjn_max_po_kernel(
 
         def load_words(name, src):
             tile = keep.tile([P, src.shape[2]], U32, name=name)
-            nc.sync.dma_start(tile[:].bitcast(I32), src[0].rearrange("p c t -> p (c t)").bitcast(I32))
+            nc.sync.dma_start(tile[:].bitcast(I32), src[0].rearrange("p c j -> p (c j)").bitcast(I32))
             return tile
 
-        def clear_scales(name, src, engine):
+        def cleared_plane(name, src, engine):
             tile = keep.tile([P, src.shape[2]], U8, name=name)
             engine.memset(tile[:].bitcast(I32), 0)
             return tile
 
         def load_scales(tile, src, queue):
-            for q in range(4):
+            for q in range(QUADRANTS):
                 queue.dma_start(tile[32 * q : 32 * q + 4, :].bitcast(I32), src[0, 4 * q : 4 * q + 4, :].bitcast(I32))
 
         def load_weight(name, src, parts):
@@ -63,26 +66,34 @@ def tile_picked_ystarjn_max_po_kernel(
                 tiles.append(tile)
             return tiles
 
-        d_table = clear_scales("d_table", d_scales, nc.vector)
-        x_table = clear_scales("x_table", x_scales, nc.vector)
-        e_table = clear_scales("e_table", e_scales, nc.gpsimd)
-        load_scales(e_table, e_scales, nc.gpsimd)
+        def empty_windows(name):
+            tiles = [keep.tile([P, S + SPARE], F32, name="%s_window%d" % (name, t)) for t in range(PACK)]
+            for tile in tiles:
+                nc.vector.memset(tile[:, S:], 0.0)
+            return tiles
+
+        e_table = cleared_plane("e_table", e_scales, nc.vector)
+        x_table = cleared_plane("x_table", x_scales, nc.vector)
+        d_table = cleared_plane("d_table", d_scales, nc.gpsimd)
+        facts, goods, shops = empty_windows("fact"), empty_windows("good"), empty_windows("shop")
+
+        load_scales(d_table, d_scales, nc.gpsimd)
         unit_sb = keep.tile([P, PACK], F32)
         nc.scalar.dma_start(unit_sb[:], unit.rearrange("(p t) o -> p (t o)", t=PACK))
-        d_sb = load_words("d_sb", d_words)
-        shp_sb = load_list("shp_sb", shp)
-        load_scales(d_table, d_scales, nc.sync)
-        w3_raw = load_weight("w3_raw", w3, 2)
-        dk2_sb = load_list("dk2_sb", dk2)
+        e_sb = load_words("e_sb", e_words)
+        prd_sb = load_list("prd_sb", prd)
+        load_scales(e_table, e_scales, nc.sync)
         x_sb = load_words("x_sb", x_words)
         offs_sb = load_list("offs_sb", offs)
         load_scales(x_table, x_scales, nc.sync)
-        w1_raw = load_weight("w1_raw", w1, 2)
+        w1_raw = load_weight("w1_raw", w1, HALVES)
         fk_sb = load_list("fk_sb", fk)
-        e_sb = load_words("e_sb", e_words)
-        prd_sb = load_list("prd_sb", prd)
-        w2_raw = load_weight("w2_raw", w2, 2)
+        w2_raw = load_weight("w2_raw", w2, HALVES)
         dk1_sb = load_list("dk1_sb", dk1)
+        d_sb = load_words("d_sb", d_words)
+        shp_sb = load_list("shp_sb", shp)
+        w3_raw = load_weight("w3_raw", w3, HALVES)
+        dk2_sb = load_list("dk2_sb", dk2)
         w4_raw = load_weight("w4_raw", w4, 1)
 
         negated = keep.tile([P, PACK], F32)
@@ -91,133 +102,123 @@ def tile_picked_ystarjn_max_po_kernel(
         nc.vector.tensor_tensor(fact_gain[:], unit_sb[:], negated[:], ALU.max)
         shop_gain = keep.tile([P, PACK], F32)
         nc.vector.tensor_tensor(shop_gain[:], unit_sb[:], negated[:], ALU.min)
-        twice = keep.tile([P, PACK], F32)
-        nc.gpsimd.tensor_scalar(twice[:], unit_sb[:], 0.0, 2.0, ALU.is_ge, ALU.mult)
+        zero_or_two = keep.tile([P, PACK], F32)
+        nc.gpsimd.tensor_scalar(zero_or_two[:], unit_sb[:], 0.0, 2.0, ALU.is_ge, ALU.mult)
         signs = keep.tile([P, PACK], F32)
-        nc.gpsimd.tensor_scalar(signs[:], twice[:], 1.0, -1.0, ALU.mult, ALU.add)
+        nc.gpsimd.tensor_scalar(signs[:], zero_or_two[:], 1.0, -1.0, ALU.mult, ALU.add)
 
-        def pick(name, words, scales, offsets):
+        def pick(name, words, table, offsets):
             codes = keep.tile([P, S], U32, name=name + "_codes", align_bytes=64)
             plane = keep.tile([P, S], U8, name=name + "_plane", align_bytes=64)
             nc.vector.tensor_copy(codes[:], words[:].indirect(offsets[:]))
-            nc.vector.tensor_copy(plane[:], scales[:].indirect(offsets[:]))
+            nc.vector.tensor_copy(plane[:], table[:].indirect(offsets[:]))
             return codes, plane
 
-        def quantise(name, raws, engines):
+        def round_signed(dealt, source):
+            rows = signs[:].unsqueeze(1).unsqueeze(3).to_broadcast([P, P, PACK, PACK])
+            nc.vector.tensor_tensor(dealt, source, rows, ALU.mult)
+
+        def quantise(name, raws, rounders):
             grouped = ring.tile([P, N * PACK], BF16, name="w_grouped", align_bytes=64)
             share = P // len(raws)
             for n, raw in enumerate(raws):
                 dealt = grouped[:].rearrange("p (t m j) -> p m j t", t=PACK, j=PACK)[:, n * share : (n + 1) * share, :, :]
-                source = raw[:].rearrange("p j (m t) -> p m j t", t=PACK)
-                if engines[n] == "x":
-                    nc.vector.tensor_tensor(dealt, source, signs[:].unsqueeze(1).unsqueeze(3).to_broadcast([P, share, PACK, PACK]), ALU.mult)
-                elif engines[n] == "s":
-                    nc.scalar.copy(dealt, source)
-                elif engines[n] == "g":
-                    nc.gpsimd.tensor_copy(dealt, source)
-                else:
-                    nc.vector.tensor_copy(dealt, source)
+                rounders[n](dealt, raw[:].rearrange("p j (m t) -> p m j t", t=PACK))
             codes = keep.tile([P, N], U32, name=name + "_wc", align_bytes=64)
             plane = keep.tile([P, N], U8, name=name + "_wp", align_bytes=64)
             nc.vector.quantize_mx(out=codes[:].bitcast(FP8X4), scales=plane[:], in_=grouped[:])
             return codes, plane
 
-        def windows(name, weight, picked, gain, engines):
-            tiles = []
-            for t in range(PACK):
-                cols = slice(t * P, (t + 1) * P)
-                bank = psum.tile([P, S], F32, name="product", bufs=4)
-                nc.tensor.matmul_mx(
-                    out=bank[:], lhsT=weight[0][:, cols].bitcast(FP8X4), lhsT_scale=weight[1][:, cols],
-                    rhs=picked[0][:].bitcast(FP8X4), rhs_scale=picked[1][:], start=True, stop=True,
-                )
-                window = keep.tile([P, S + SPARE], F32, name="%s_window%d" % (name, t))
-                if SPARE:
-                    nc.gpsimd.memset(window[:, S:], 0.0)
-                if gain is None:
-                    if engines[t] == "s":
-                        nc.scalar.activation(window[:, :S], bank[:], COPY)
-                    else:
-                        nc.vector.tensor_copy(window[:, :S], bank[:])
-                elif engines[t] == "s":
-                    nc.scalar.activation(window[:, :S], bank[:], COPY, scale=gain[:, t : t + 1])
-                else:
-                    nc.vector.tensor_scalar(window[:, :S], bank[:], gain[:, t : t + 1], None, ALU.mult)
-                tiles.append(window)
-            return tiles
+        def product(weight, picked, t):
+            cols = slice(t * P, (t + 1) * P)
+            bank = psum.tile([P, S], F32, name="product")
+            nc.tensor.matmul_mx(
+                out=bank[:], lhsT=weight[0][:, cols].bitcast(FP8X4), lhsT_scale=weight[1][:, cols],
+                rhs=picked[0][:].bitcast(FP8X4), rhs_scale=picked[1][:], start=True, stop=True,
+            )
+            return bank
 
-        d_pick = pick("d", d_sb, d_table, shp_sb)
-        shops = windows("shop", quantise("w3", w3_raw, "sv"), d_pick, shop_gain, "ssss")
-        x_pick = pick("x", x_sb, x_table, offs_sb)
-        facts = windows("fact", quantise("w1", w1_raw, "vv"), x_pick, fact_gain, "ssss")
+        def scaled_windows(windows, weight, picked, gain):
+            for t in range(PACK):
+                nc.scalar.activation(windows[t][:, :S], product(weight, picked, t)[:], COPY, scale=gain[:, t : t + 1])
+
+        on_vector = [nc.vector.tensor_copy] * HALVES
         e_pick = pick("e", e_sb, e_table, prd_sb)
-        goods = windows("good", quantise("w2", w2_raw, "vv"), e_pick, None, "ssss")
+        x_pick = pick("x", x_sb, x_table, offs_sb)
+        scaled_windows(facts, quantise("w1", w1_raw, [nc.scalar.copy, nc.vector.tensor_copy]), x_pick, fact_gain)
+        w2_q = quantise("w2", w2_raw, on_vector)
+        for t in range(PACK):
+            if t < GOODS_BANKS_ON_VECTOR:
+                nc.vector.tensor_copy(goods[t][:, :S], product(w2_q, e_pick, t)[:])
+            else:
+                nc.scalar.activation(goods[t][:, :S], product(w2_q, e_pick, t)[:], COPY)
+        d_pick = pick("d", d_sb, d_table, shp_sb)
+        scaled_windows(shops, quantise("w3", w3_raw, on_vector), d_pick, shop_gain)
 
         out_codes = keep.tile([P, U], U32, align_bytes=64)
         out_plane = keep.tile([P, U], U8, align_bytes=64)
 
-        def join(c, start, width):
-            entries = slice(start // 16, (start + width) // 16)
-            fact = ring.tile([P, PACK, width], F32, name="fact", bufs=2)
-            less = ring.tile([P, PACK, width], F32, name="less", bufs=2)
-            more = ring.tile([P, PACK, width], F32, name="more", bufs=2)
+        def join(start, width):
+            entries = slice(start // LIST_ROWS, (start + width) // LIST_ROWS)
+            fact = ring.tile([P, PACK, width], F32, name="fact")
+            differ = ring.tile([P, PACK, width], F32, name="differ")
+            joined = ring.tile([P, PACK, width], F32, name="joined")
             for t in range(PACK):
                 nc.scalar.activation(fact[:, t, :], facts[t][:].indirect(fk_sb[:, entries]), COPY)
             for t in range(PACK):
-                nc.scalar.activation(less[:, t, :], shops[t][:].indirect(dk2_sb[:, entries]), COPY)
+                nc.scalar.activation(differ[:, t, :], shops[t][:].indirect(dk2_sb[:, entries]), COPY)
             for t in range(PACK):
-                nc.vector.tensor_tensor(more[:, t, :], goods[t][:].indirect(dk1_sb[:, entries]), fact[:, t, :], ALU.mult)
-            nc.vector.scalar_tensor_tensor(more[:], less[:], -SHOP, more[:], ALU.mult, ALU.add)
-            nc.vector.tensor_tensor(less[:], less[:], fact[:], ALU.add)
+                nc.vector.tensor_tensor(joined[:, t, :], goods[t][:].indirect(dk1_sb[:, entries]), fact[:, t, :], ALU.mult)
+            nc.vector.scalar_tensor_tensor(joined[:], differ[:], -SHOP, joined[:], ALU.mult, ALU.add)
+            nc.vector.tensor_tensor(differ[:], differ[:], fact[:], ALU.add)
             hid = ring.tile([P, width * PACK], BF16, name="hid", align_bytes=64)
             walk = "p t (c i) -> p c t i"
             nc.vector.tensor_tensor(
-                hid[:].rearrange("p (c i t) -> p c t i", i=4, t=PACK), more[:].rearrange(walk, i=4), less[:].rearrange(walk, i=4), ALU.max
+                hid[:].rearrange("p (c i t) -> p c t i", i=LINE, t=PACK),
+                joined[:].rearrange(walk, i=LINE),
+                differ[:].rearrange(walk, i=LINE),
+                ALU.max,
             )
             codes = ring.tile([P, width], U32, name="hid_codes", align_bytes=64)
             plane = ring.tile([P, width], U8, name="hid_plane", align_bytes=64)
             nc.vector.quantize_mx(out=codes[:].bitcast(FP8X4), scales=plane[:], in_=hid[:])
             return codes, plane
 
-        def finish(c, start, width, codes, plane):
-            result = ring.tile([P, PACK, width], F32, name="result", bufs=2)
+        def finish(start, width, codes, plane, rounder):
+            result = ring.tile([P, PACK, width], F32, name="result", bufs=len(CHUNKS))
             rounded = ring.tile([P, width * PACK], BF16, name="rounded", align_bytes=64)
-            for b in range(width // P):
+            blocks = width // P
+            for b in range(blocks):
                 cols = slice(b * P, (b + 1) * P)
-                bank = psum.tile([P, PACK, P], F32, name="measure", bufs=4)
+                bank = psum.tile([P, PACK, P], F32, name="measure")
                 for t in range(PACK):
                     rows = slice(t * P, (t + 1) * P)
                     nc.tensor.matmul_mx(
                         out=bank[:, t, :], lhsT=w4_q[0][:, rows].bitcast(FP8X4), lhsT_scale=w4_q[1][:, rows],
                         rhs=codes[:, cols].bitcast(FP8X4), rhs_scale=plane[:, cols], start=True, stop=True,
                     )
-                if c not in VCAST:
-                    nc.scalar.copy(
-                        rounded[:, b * S : (b + 1) * S].rearrange("p (r t) -> p r t", t=PACK), bank[:].rearrange("p t r -> p r t")
+                words = rounded[:, b * P * PACK : (b + 1) * P * PACK]
+                rounder(words.rearrange("p (r t) -> p r t", t=PACK), bank[:].rearrange("p t r -> p r t"))
+                nc.scalar.copy(result[:, :, cols], bank[:])
+                if (b + 1) % STORE_BLOCKS == 0 or b + 1 == blocks:
+                    first = b // STORE_BLOCKS * STORE_BLOCKS * P
+                    nc.sync.dma_start(
+                        out_0.rearrange("(p t) r -> p t r", t=PACK)[:, :, start + first : start + (b + 1) * P],
+                        result[:, :, first : (b + 1) * P],
                     )
-                if c in VEVAC:
-                    nc.vector.tensor_copy(result[:, :, cols], bank[:])
-                else:
-                    nc.scalar.copy(result[:, :, cols], bank[:])
-            cols = slice(start, start + width)
-            nc.sync.dma_start(out_0.rearrange("(p t) r -> p t r", t=PACK)[:, :, cols], result[:])
-            if c in VCAST:
-                nc.vector.tensor_copy(
-                    rounded[:].rearrange("p (c i t) -> p c t i", i=4, t=PACK), result[:].rearrange("p t (c i) -> p c t i", i=4)
-                )
-            nc.vector.quantize_mx(out=out_codes[:, cols].bitcast(FP8X4), scales=out_plane[:, cols], in_=rounded[:])
+            chunk = slice(start, start + width)
+            nc.vector.quantize_mx(out=out_codes[:, chunk].bitcast(FP8X4), scales=out_plane[:, chunk], in_=rounded[:])
             nc.sync.dma_start(
-                out_1[0].rearrange("p c t -> p (c t)")[:, PACK * start : PACK * (start + width)].bitcast(I32),
-                out_codes[:, cols].bitcast(I32),
+                out_1[0].rearrange("p c j -> p (c j)")[:, PACK * start : PACK * (start + width)].bitcast(I32),
+                out_codes[:, chunk].bitcast(I32),
             )
 
         start = 0
         for c, width in enumerate(CHUNKS):
-            codes, plane = join(c, start, width)
+            codes, plane = join(start, width)
             if c == 0:
-                w4_q = quantise("w4", w4_raw, "x")
-            finish(c, start, width, codes, plane)
+                w4_q = quantise("w4", w4_raw, [round_signed])
+            finish(start, width, codes, plane, nc.vector.tensor_copy if c + 1 == len(CHUNKS) else nc.scalar.copy)
             start = start + width
-        for q in range(4):
-            queue = nc.sync if q % 2 == 0 else nc.scalar
-            queue.dma_start(out_2[0, 4 * q : 4 * q + 4, :].bitcast(I32), out_plane[32 * q : 32 * q + 4, :].bitcast(I32))
+        for q in range(QUADRANTS):
+            nc.sync.dma_start(out_2[0, 4 * q : 4 * q + 4, :].bitcast(I32), out_plane[32 * q : 32 * q + 4, :].bitcast(I32))

from contextlib import ExitStack

import concourse.mybir as mybir

K, S, N, H, U = 512, 512, 512, 512, 1024
FLOPS = 2 * (3 * K * H * S + H * N * U)

F32 = mybir.dt.float32
BF16 = mybir.dt.bfloat16
I32 = mybir.dt.int32
U32 = mybir.dt.uint32
U16 = mybir.dt.uint16
U8 = mybir.dt.uint8
FP8X4 = mybir.dt.float8_e4m3fn_x4
ALU = mybir.AluOpType
COPY = mybir.ActivationFunctionType.Copy

P = 128
PACK = 4
LINE = 4
LIST_ROWS = 16
QUADRANTS = 4
SHOP = 0.7
SPARE = 16
HALVES = 2
CHUNKS = (256, 512, 128, 128)
STORE_BLOCKS = 2
GOODS_BANKS_ON_VECTOR = 3


def tile_picked_ystarjn_max_po_kernel(
    tc, x_words, x_scales, w1, e_words, e_scales, w2, d_words, d_scales, w3, unit, w4,
    offs, prd, shp, fk, dk1, dk2, out_0, out_1, out_2,
):
    nc = tc.nc
    with ExitStack() as ctx:
        keep = ctx.enter_context(tc.tile_pool(name="keep", bufs=1))
        ring = ctx.enter_context(tc.tile_pool(name="ring", bufs=2))
        psum = ctx.enter_context(tc.psum_pool(name="psum", bufs=4))

        def load_list(name, src):
            tile = keep.tile(list(src.shape), U16, name=name)
            nc.sync.dma_start(tile[:], src)
            return tile

        def load_words(name, src):
            tile = keep.tile([P, src.shape[2]], U32, name=name)
            nc.sync.dma_start(tile[:].bitcast(I32), src[0].rearrange("p c j -> p (c j)").bitcast(I32))
            return tile

        def cleared_plane(name, src, engine):
            tile = keep.tile([P, src.shape[2]], U8, name=name)
            engine.memset(tile[:].bitcast(I32), 0)
            return tile

        def load_scales(tile, src, queue):
            for q in range(QUADRANTS):
                queue.dma_start(tile[32 * q : 32 * q + 4, :].bitcast(I32), src[0, 4 * q : 4 * q + 4, :].bitcast(I32))

        def load_weight(name, src, parts):
            tiles = []
            width = N // parts
            for n in range(parts):
                tile = keep.tile([P, PACK, width], F32, name="%s%d" % (name, n))
                nc.sync.dma_start(tile[:], src.rearrange("(p j) c -> p j c", j=PACK)[:, :, n * width : (n + 1) * width])
                tiles.append(tile)
            return tiles

        def empty_windows(name):
            tiles = [keep.tile([P, S + SPARE], F32, name="%s_window%d" % (name, t)) for t in range(PACK)]
            for tile in tiles:
                nc.vector.memset(tile[:, S:], 0.0)
            return tiles

        e_table = cleared_plane("e_table", e_scales, nc.vector)
        x_table = cleared_plane("x_table", x_scales, nc.vector)
        d_table = cleared_plane("d_table", d_scales, nc.gpsimd)
        facts, goods, shops = empty_windows("fact"), empty_windows("good"), empty_windows("shop")

        load_scales(d_table, d_scales, nc.gpsimd)
        unit_sb = keep.tile([P, PACK], F32)
        nc.scalar.dma_start(unit_sb[:], unit.rearrange("(p t) o -> p (t o)", t=PACK))
        e_sb = load_words("e_sb", e_words)
        prd_sb = load_list("prd_sb", prd)
        load_scales(e_table, e_scales, nc.sync)
        x_sb = load_words("x_sb", x_words)
        offs_sb = load_list("offs_sb", offs)
        load_scales(x_table, x_scales, nc.sync)
        w1_raw = load_weight("w1_raw", w1, HALVES)
        fk_sb = load_list("fk_sb", fk)
        w2_raw = load_weight("w2_raw", w2, HALVES)
        dk1_sb = load_list("dk1_sb", dk1)
        d_sb = load_words("d_sb", d_words)
        shp_sb = load_list("shp_sb", shp)
        w3_raw = load_weight("w3_raw", w3, HALVES)
        dk2_sb = load_list("dk2_sb", dk2)
        w4_raw = load_weight("w4_raw", w4, 1)

        negated = keep.tile([P, PACK], F32)
        nc.scalar.activation(negated[:], unit_sb[:], COPY, scale=-1.0)
        fact_gain = keep.tile([P, PACK], F32)
        nc.vector.tensor_tensor(fact_gain[:], unit_sb[:], negated[:], ALU.max)
        shop_gain = keep.tile([P, PACK], F32)
        nc.vector.tensor_tensor(shop_gain[:], unit_sb[:], negated[:], ALU.min)
        zero_or_two = keep.tile([P, PACK], F32)
        nc.gpsimd.tensor_scalar(zero_or_two[:], unit_sb[:], 0.0, 2.0, ALU.is_ge, ALU.mult)
        signs = keep.tile([P, PACK], F32)
        nc.gpsimd.tensor_scalar(signs[:], zero_or_two[:], 1.0, -1.0, ALU.mult, ALU.add)

        def pick(name, words, table, offsets):
            codes = keep.tile([P, S], U32, name=name + "_codes", align_bytes=64)
            plane = keep.tile([P, S], U8, name=name + "_plane", align_bytes=64)
            nc.vector.tensor_copy(codes[:], words[:].indirect(offsets[:]))
            nc.vector.tensor_copy(plane[:], table[:].indirect(offsets[:]))
            return codes, plane

        def round_signed(dealt, source):
            rows = signs[:].unsqueeze(1).unsqueeze(3).to_broadcast([P, P, PACK, PACK])
            nc.vector.tensor_tensor(dealt, source, rows, ALU.mult)

        def quantise(name, raws, rounders):
            grouped = ring.tile([P, N * PACK], BF16, name="w_grouped", align_bytes=64)
            share = P // len(raws)
            for n, raw in enumerate(raws):
                dealt = grouped[:].rearrange("p (t m j) -> p m j t", t=PACK, j=PACK)[:, n * share : (n + 1) * share, :, :]
                rounders[n](dealt, raw[:].rearrange("p j (m t) -> p m j t", t=PACK))
            codes = keep.tile([P, N], U32, name=name + "_wc", align_bytes=64)
            plane = keep.tile([P, N], U8, name=name + "_wp", align_bytes=64)
            nc.vector.quantize_mx(out=codes[:].bitcast(FP8X4), scales=plane[:], in_=grouped[:])
            return codes, plane

        def product(weight, picked, t):
            cols = slice(t * P, (t + 1) * P)
            bank = psum.tile([P, S], F32, name="product")
            nc.tensor.matmul_mx(
                out=bank[:], lhsT=weight[0][:, cols].bitcast(FP8X4), lhsT_scale=weight[1][:, cols],
                rhs=picked[0][:].bitcast(FP8X4), rhs_scale=picked[1][:], start=True, stop=True,
            )
            return bank

        def scaled_windows(windows, weight, picked, gain):
            for t in range(PACK):
                nc.scalar.activation(windows[t][:, :S], product(weight, picked, t)[:], COPY, scale=gain[:, t : t + 1])

        on_vector = [nc.vector.tensor_copy] * HALVES
        e_pick = pick("e", e_sb, e_table, prd_sb)
        x_pick = pick("x", x_sb, x_table, offs_sb)
        scaled_windows(facts, quantise("w1", w1_raw, [nc.scalar.copy, nc.vector.tensor_copy]), x_pick, fact_gain)
        w2_q = quantise("w2", w2_raw, on_vector)
        for t in range(PACK):
            if t < GOODS_BANKS_ON_VECTOR:
                nc.vector.tensor_copy(goods[t][:, :S], product(w2_q, e_pick, t)[:])
            else:
                nc.scalar.activation(goods[t][:, :S], product(w2_q, e_pick, t)[:], COPY)
        d_pick = pick("d", d_sb, d_table, shp_sb)
        scaled_windows(shops, quantise("w3", w3_raw, on_vector), d_pick, shop_gain)

        out_codes = keep.tile([P, U], U32, align_bytes=64)
        out_plane = keep.tile([P, U], U8, align_bytes=64)

        def join(start, width):
            entries = slice(start // LIST_ROWS, (start + width) // LIST_ROWS)
            fact = ring.tile([P, PACK, width], F32, name="fact")
            differ = ring.tile([P, PACK, width], F32, name="differ")
            joined = ring.tile([P, PACK, width], F32, name="joined")
            for t in range(PACK):
                nc.scalar.activation(fact[:, t, :], facts[t][:].indirect(fk_sb[:, entries]), COPY)
            for t in range(PACK):
                nc.scalar.activation(differ[:, t, :], shops[t][:].indirect(dk2_sb[:, entries]), COPY)
            for t in range(PACK):
                nc.vector.tensor_tensor(joined[:, t, :], goods[t][:].indirect(dk1_sb[:, entries]), fact[:, t, :], ALU.mult)
            nc.vector.scalar_tensor_tensor(joined[:], differ[:], -SHOP, joined[:], ALU.mult, ALU.add)
            nc.vector.tensor_tensor(differ[:], differ[:], fact[:], ALU.add)
            hid = ring.tile([P, width * PACK], BF16, name="hid", align_bytes=64)
            walk = "p t (c i) -> p c t i"
            nc.vector.tensor_tensor(
                hid[:].rearrange("p (c i t) -> p c t i", i=LINE, t=PACK),
                joined[:].rearrange(walk, i=LINE),
                differ[:].rearrange(walk, i=LINE),
                ALU.max,
            )
            codes = ring.tile([P, width], U32, name="hid_codes", align_bytes=64)
            plane = ring.tile([P, width], U8, name="hid_plane", align_bytes=64)
            nc.vector.quantize_mx(out=codes[:].bitcast(FP8X4), scales=plane[:], in_=hid[:])
            return codes, plane

        def finish(start, width, codes, plane, rounder):
            result = ring.tile([P, PACK, width], F32, name="result", bufs=len(CHUNKS))
            rounded = ring.tile([P, width * PACK], BF16, name="rounded", align_bytes=64)
            blocks = width // P
            for b in range(blocks):
                cols = slice(b * P, (b + 1) * P)
                bank = psum.tile([P, PACK, P], F32, name="measure")
                for t in range(PACK):
                    rows = slice(t * P, (t + 1) * P)
                    nc.tensor.matmul_mx(
                        out=bank[:, t, :], lhsT=w4_q[0][:, rows].bitcast(FP8X4), lhsT_scale=w4_q[1][:, rows],
                        rhs=codes[:, cols].bitcast(FP8X4), rhs_scale=plane[:, cols], start=True, stop=True,
                    )
                words = rounded[:, b * P * PACK : (b + 1) * P * PACK]
                rounder(words.rearrange("p (r t) -> p r t", t=PACK), bank[:].rearrange("p t r -> p r t"))
                nc.scalar.copy(result[:, :, cols], bank[:])
                if (b + 1) % STORE_BLOCKS == 0 or b + 1 == blocks:
                    first = b // STORE_BLOCKS * STORE_BLOCKS * P
                    nc.sync.dma_start(
                        out_0.rearrange("(p t) r -> p t r", t=PACK)[:, :, start + first : start + (b + 1) * P],
                        result[:, :, first : (b + 1) * P],
                    )
            chunk = slice(start, start + width)
            nc.vector.quantize_mx(out=out_codes[:, chunk].bitcast(FP8X4), scales=out_plane[:, chunk], in_=rounded[:])
            nc.sync.dma_start(
                out_1[0].rearrange("p c j -> p (c j)")[:, PACK * start : PACK * (start + width)].bitcast(I32),
                out_codes[:, chunk].bitcast(I32),
            )

        start = 0
        for c, width in enumerate(CHUNKS):
            codes, plane = join(start, width)
            if c == 0:
                w4_q = quantise("w4", w4_raw, [round_signed])
            finish(start, width, codes, plane, nc.vector.tensor_copy if c + 1 == len(CHUNKS) else nc.scalar.copy)
            start = start + width
        for q in range(QUADRANTS):
            nc.sync.dma_start(out_2[0, 4 * q : 4 * q + 4, :].bitcast(I32), out_plane[32 * q : 32 * q + 4, :].bitcast(I32))
